import numpy as np
import ml_dtypes


def mxq(x, axis, fmt="e4m3"):
    dtype, down = {"e4m3": (ml_dtypes.float8_e4m3fn, 7), "e5m2": (ml_dtypes.float8_e5m2, 14)}[fmt]
    v = np.moveaxis(np.asarray(x, np.float32).astype(ml_dtypes.bfloat16).astype(np.float64), axis, -1)
    blocks = v.reshape(v.shape[:-1] + (-1, 32))
    amax = np.abs(blocks).max(-1, keepdims=True)
    byte = np.maximum(np.where(amax > 0, np.frexp(amax)[1] - 1 + 127, 0) - down, 1)
    scale = np.exp2(byte - 127.0)
    codes = (blocks / scale).astype(np.float32).astype(dtype).astype(np.float64)
    return np.moveaxis((codes * scale).reshape(v.shape), -1, axis)


WIDE = False


def mx_kscale(k):
    if not WIDE:
        return np.ones(k)
    levels = np.array([10, -10, 5, -5, 0])
    if k % 512:
        return np.exp2(np.random.permutation(np.resize(levels, k // 32))).repeat(32)
    a = np.empty((k // 512, 16))
    for p in range(k // 512):
        a[p, :8] = np.random.permutation(np.resize(levels, 8))
        for g in range(8):
            far = levels[np.abs(levels - a[p, g]) >= 10]
            a[p, g + 8] = far[np.random.randint(len(far))]
    return np.exp2(a.ravel()).repeat(32)


BF16 = ml_dtypes.bfloat16


def bf(x):
    return np.asarray(x, np.float32).astype(BF16)


def f64(x):
    return np.asarray(x).astype(np.float64)


E2M1 = np.array([0.0, 0.5, 1.0, 1.5, 2.0, 3.0, 4.0, 6.0, -0.0, -0.5, -1.0, -1.5, -2.0, -3.0, -4.0, -6.0])


def pack_weight(w, fmt):
    k, n = w.shape
    w = f64(bf(w)).reshape(k // 32, 32, n)
    amax = np.abs(w).max(1)
    if fmt == "e4m3":
        byte = np.frexp(amax)[1] - 1 + 127 - 7
    else:
        mant, ex = np.frexp(amax / 6.0)
        byte = np.where(mant > 0.5, ex, ex - 1) + 127
    byte = np.clip(np.where(amax > 0, byte, 1), 1, 254)
    scaled = (w * np.exp2(127.0 - byte)[:, None, :]).reshape(k, n).astype(np.float32)
    by_word = np.ascontiguousarray(scaled.reshape(k // 512, 128, 4, n).transpose(0, 1, 3, 2))
    if fmt == "e4m3":
        words = by_word.astype(ml_dtypes.float8_e4m3fn).view(np.uint8)
    else:
        c = by_word.astype(ml_dtypes.float4_e2m1fn).view(np.uint8) & 0xF
        words = c[..., 0::2] | (c[..., 1::2] << 4)
    return np.ascontiguousarray(words), np.ascontiguousarray(byte.astype(np.uint8).reshape(k // 512, 16, n))


def unpack_weight(words, scales, fmt):
    g, p, n, _ = words.shape
    if fmt == "e4m3":
        vals = np.ascontiguousarray(words).view(ml_dtypes.float8_e4m3fn).astype(np.float64)
    else:
        nib = np.empty((g, p, n, 4), np.uint8)
        nib[..., 0::2] = words & 0xF
        nib[..., 1::2] = words >> 4
        vals = E2M1[nib]
    vals = vals * np.repeat(np.exp2(scales.astype(np.float64) - 127.0), 8, axis=1)[..., None]
    return vals.transpose(0, 1, 3, 2).reshape(g * 512, n)
def pack4(w):
    words, scales = pack_weight(w, "e2m1")
    return words.reshape(words.shape[0], 128, -1), scales


def unpack4(words, scales):
    return unpack_weight(words.reshape(words.shape[0], 128, -1, 2), scales, "e2m1")


B, KO, KR, F, J = 1024, 512, 2048, 1024, 1024

OUTLIER = 4.0
SPREAD = 0.45


def draw0():
    u, s, t = mx_kscale(KO), mx_kscale(KR), mx_kscale(F)
    base = SPREAD * np.random.standard_normal((KR, F)) / np.sqrt(KR)
    proj = np.random.standard_normal((F, J)) / np.sqrt(F)
    base_words, base_scales = pack4(base / s[:, None])
    proj_words, proj_scales = pack4(proj / t[:, None])
    online = 0.1 + np.random.exponential(size=(B, J))
    return {"x_out": bf(OUTLIER * np.random.standard_normal((B, KO)) * u),
            "w_out": bf(SPREAD / OUTLIER * np.random.standard_normal((KO, F)) / np.sqrt(KO) / u[:, None]),
            "x_rest": bf(np.random.standard_normal((B, KR)) * s),
            "base_words": base_words,
            "base_scales": base_scales,
            "spacing": bf((1 + 0.1 * np.random.standard_normal(F)) * t),
            "proj_words": proj_words,
            "proj_scales": proj_scales,
            "online": bf(online / online.sum(axis=1, keepdims=True))}


def core(x_out, w_out, x_rest, base_words, base_scales, spacing, proj_words, proj_scales, online):
    z = ((mxq(f64(x_out), 1, "e4m3") @ mxq(f64(w_out), 0, "e4m3"))
         + (mxq(f64(x_rest), 1, "e4m3") @ unpack4(base_words, base_scales)))
    mass = np.exp(z) * f64(spacing)
    target = mxq(mass, 1, "e4m3") @ unpack4(proj_words, proj_scales)
    loss = -np.mean(target * np.log(f64(online)), axis=1)
    return target, loss


def e4m3fn_bytes(y):
    return np.clip(np.asarray(y, np.float64), -448.0, 448.0).astype(np.float32).astype(ml_dtypes.float8_e4m3fn).view(np.uint8)


def e4m3fn_values(b):
    return np.asarray(b, np.uint8).view(ml_dtypes.float8_e4m3fn).astype(np.float64)


def setup_inputs():
    d = draw0()
    x0 = np.asarray(d['x_rest']).astype(np.float64)
    s = (np.max(np.abs(x0), axis=(0,), keepdims=True) / 448.0).astype(np.float32)
    out = {}
    for k, v in d.items():
        if k == 'x_rest':
            out['x_rest_bytes'] = e4m3fn_bytes(x0 / s.astype(np.float64))
            out['x_rest_scale'] = s
        else:
            out[k] = v
    return out


def reference(x_out, w_out, x_rest_bytes, x_rest_scale, base_words, base_scales, spacing, proj_words, proj_scales, online):
    return core(x_out, w_out, e4m3fn_values(x_rest_bytes) * x_rest_scale.astype(np.float64), base_words, base_scales, spacing, proj_words, proj_scales, online)

@@ -1,0 +1,511 @@
+from contextlib import ExitStack
+
+import concourse.mybir as mybir
+from concourse.masks import make_identity
+
+B, KO, KR, F, J = 1024, 512, 2048, 1024, 1024
+FLOPS = 2 * B * F * (KO + KR) + 2 * B * J * F
+
+F32 = mybir.dt.float32
+BF16 = mybir.dt.bfloat16
+I32 = mybir.dt.int32
+U32 = mybir.dt.uint32
+U8 = mybir.dt.uint8
+FP8 = mybir.dt.float8_e4m3fn
+FP8X4 = mybir.dt.float8_e4m3fn_x4
+FP4X4 = mybir.dt.float4_e2m1fn_x4
+ACT = mybir.ActivationFunctionType
+ALU = mybir.AluOpType
+
+P = 128
+NT = B // P
+HALF = 512
+GR = KR // 512
+GM = F // 512
+
+
+def tile_c51_shifted_log_loss_s3_kernel(
+    tc, x_out, w_out, x_rest_bytes, x_rest_scale, base_words, base_scales, spacing, proj_words, proj_scales, online, target, loss
+):
+    nc = tc.nc
+    with ExitStack() as ctx:
+        keep = ctx.enter_context(tc.tile_pool(name="keep", bufs=1))
+        work = ctx.enter_context(tc.tile_pool(name="work", bufs=3))
+        psum = ctx.enter_context(tc.psum_pool(name="psum", bufs=4))
+
+        def kept(shape, dtype, name):
+            return keep.tile(shape, dtype, name=name, tag=name, align_bytes=64)
+
+        xr = [kept([P, KR], U8, "xr%d" % i) for i in range(NT)]
+        sc = kept([P, GR, 2, 2], F32, "sc")
+        base = kept([P, GR, 2 * F], U8, "base")
+        bsc = kept([P, GR, F], U8, "bsc")
+        proj = kept([P, GM, 2 * J], U8, "proj")
+        psc = kept([P, GM, J], U8, "psc")
+        wraw = kept([P, 4, F], BF16, "wraw")
+        wgrp = [kept([P, HALF, 4], BF16, "wgrp%d" % h) for h in range(2)]
+        wcod = [kept([P, HALF], U32, "wcod%d" % h) for h in range(2)]
+        wscl = [kept([P, HALF], U8, "wscl%d" % h) for h in range(2)]
+        xo = [kept([P, 2, KO], BF16, "xo%d" % i) for i in range(NT // 2)]
+        onl = [kept([P, 2, J], BF16, "onl%d" % i) for i in range(NT // 2)]
+        logs = kept([P, NT, J], F32, "logs")
+        spc = kept([P, F], BF16, "spc")
+        ident = kept([P, P], F32, "ident")
+        acc = [kept([P, NT], F32, "acc%d" % h) for h in range(2)]
+        lpad = kept([P, P], F32, "lpad")
+        lrow = kept([32, P], F32, "lrow")
+        one = kept([P, 1], F32, "one")
+        junk1 = kept([P, 1], F32, "junk1")
+        xcod = [kept([P, GR, P], U32, "xcod%d" % i) for i in range(NT)]
+        xscl = [kept([P, GR, P], U8, "xscl%d" % i) for i in range(NT)]
+        ocod = [kept([P, 2, P], U32, "ocod%d" % i) for i in range(NT // 2)]
+        oscl = [kept([P, 2, P], U8, "oscl%d" % i) for i in range(NT // 2)]
+
+        if True:
+            nc.vector.memset(one[:], 1.0)
+            nc.vector.memset(bsc[:].rearrange("p g n -> p (g n)").bitcast(I32), 0)
+            nc.vector.memset(psc[:].rearrange("p g n -> p (g n)").bitcast(I32), 0)
+            nc.vector.memset(lpad[:], 0.0)
+            nc.scalar.activation(out=junk1[:], in_=one[:], func=ACT.Ln)
+            make_identity(nc, ident[:])
+
+            def load_x(i):
+                nc.sync.dma_start(out=xr[i][:], in_=x_rest_bytes[P * i : P * (i + 1), :])
+
+            def load_onl(a):
+                nc.sync.dma_start(out=onl[a][:], in_=online[2 * P * a : 2 * P * (a + 1), :].rearrange("(i r) j -> r i j", r=P))
+
+            def load_xo(a):
+                nc.sync.dma_start(out=xo[a][:], in_=x_out[2 * P * a : 2 * P * (a + 1), :].rearrange("(i r) k -> r i k", r=P))
+
+            load_x(0)
+            nc.sync.dma_start(out=sc[:].rearrange("p g u e -> p g (u e)"), in_=x_rest_scale.rearrange("o (g p t) -> p (o g) t", p=P, t=4))
+            load_x(1)
+            load_onl(0)
+            for q in range(4):
+                nc.sync.dma_start(
+                    out=bsc[32 * q : 32 * q + 4].bitcast(I32),
+                    in_=base_scales[:, 4 * q : 4 * q + 4, :].rearrange("g r n -> r g n").bitcast(I32),
+                )
+            nc.sync.dma_start(out=base[:], in_=base_words.rearrange("g p n -> p g n"))
+            load_x(2)
+            load_onl(1)
+            nc.sync.dma_start(out=wraw[:], in_=w_out.rearrange("(p j) n -> p j n", j=4))
+            load_x(3)
+            load_xo(0)
+            load_onl(2)
+            load_onl(3)
+            load_x(4)
+            for q in range(4):
+                nc.sync.dma_start(
+                    out=psc[32 * q : 32 * q + 4].bitcast(I32),
+                    in_=proj_scales[:, 4 * q : 4 * q + 4, :].rearrange("g r n -> r g n").bitcast(I32),
+                )
+            nc.sync.dma_start(out=spc[:], in_=spacing.partition_broadcast(P))
+            load_xo(1)
+            load_x(5)
+            nc.sync.dma_start(out=proj[:], in_=proj_words.rearrange("g p n -> p g n"))
+            load_x(6)
+            load_xo(2)
+            load_x(7)
+            load_xo(3)
+
+            wide = {}
+            xt = {}
+            grp = {}
+            z = {}
+            ex = {}
+            mass = {}
+            mt = {}
+            mgrp = {}
+            mcod = {}
+            mscl = {}
+            tg = {}
+            tout = {}
+
+            def cast(i):
+                t = work.tile([P, KR], BF16, name="wide", tag="wide", bufs=4)
+                wide[i] = t
+                if i < 2:
+                    nc.scalar.copy(out=t[:, 0:512], in_=xr[i][:, 0:512].bitcast(FP8))
+                    nc.vector.tensor_copy(out=t[:, 512:1024], in_=xr[i][:, 512:1024].bitcast(FP8))
+                    nc.vector.tensor_copy(out=t[:, 1024:2048], in_=xr[i][:, 1024:2048].bitcast(FP8))
+                else:
+                    nc.scalar.copy(out=t[:], in_=xr[i][:].bitcast(FP8))
+
+            def xtrans(i, b):
+                t = psum.tile([P, 2, 2, P], F32, name="xt", tag="xt", bufs=4)
+                xt[i, b] = t
+                words = wide[i][:].bitcast(F32)
+                for gg in range(2):
+                    g = 2 * b + gg
+                    for u in range(2):
+                        nc.tensor.transpose(t[:, u, gg, :], words[:, 256 * g + u : 256 * (g + 1) : 2], ident[:])
+
+            def prod(i, b):
+                if b == 0:
+                    grp[i] = work.tile([P, GR, P, 2, 2], BF16, name="grp", tag="grp", bufs=4, align_bytes=64)
+                t = xt[i, b][:].rearrange("p u g r -> p (u g r)").bitcast(BF16).rearrange("p (u g r e) -> p g r u e", u=2, g=2, e=2)
+                s = sc[:, 2 * b : 2 * b + 2].unsqueeze(2).to_broadcast([P, 2, P, 2, 2])
+                nc.vector.tensor_tensor(out=grp[i][:, 2 * b : 2 * b + 2], in0=t, in1=s, op=ALU.mult)
+
+            def xquant(i):
+                nc.vector.quantize_mx(
+                    out=xcod[i][:].rearrange("p g r -> p (g r)").bitcast(FP8X4),
+                    scales=xscl[i][:].rearrange("p g r -> p (g r)"),
+                    in_=grp[i][:].rearrange("p g r u e -> p (g r u e)"),
+                )
+
+            def otrans(a):
+                t = psum.tile([P, 2, 2, P], F32, name="xt", tag="xt", bufs=4)
+                xt["o", a] = t
+                for i in range(2):
+                    words = xo[a][:, i, :].bitcast(F32)
+                    for u in range(2):
+                        nc.tensor.transpose(t[:, u, i, :], words[:, u::2], ident[:])
+
+            def oexit(a):
+                grp["o", a] = work.tile([P, 2 * P * 4], BF16, name="ogrp", tag="ogrp", bufs=2, align_bytes=64)
+                nc.vector.tensor_copy(
+                    out=grp["o", a][:].bitcast(F32).rearrange("p (i r u) -> p i r u", i=2, u=2),
+                    in_=xt["o", a][:].rearrange("p u i r -> p i r u"),
+                )
+
+            def oquant(a):
+                nc.vector.quantize_mx(
+                    out=ocod[a][:].rearrange("p i r -> p (i r)").bitcast(FP8X4),
+                    scales=oscl[a][:].rearrange("p i r -> p (i r)"),
+                    in_=grp["o", a][:],
+                )
+
+            def wgroup(h):
+                nc.gpsimd.tensor_scalar(
+                    out=wgrp[h][:],
+                    in0=wraw[:, :, HALF * h : HALF * (h + 1)].rearrange("p j n -> p n j"),
+                    scalar1=1.0,
+                    scalar2=0.0,
+                    op0=ALU.mult,
+                    op1=ALU.add,
+                )
+
+            def wquant(h):
+                nc.vector.quantize_mx(out=wcod[h][:].bitcast(FP8X4), scales=wscl[h][:], in_=wgrp[h][:].rearrange("p n j -> p (n j)"))
+
+            def zrest(i, h):
+                t = psum.tile([P, HALF], F32, name="mm", tag="mm", bufs=4)
+                z[i, h] = t
+                for g in range(GR):
+                    nc.tensor.matmul_mx(
+                        out=t[:],
+                        lhsT=xcod[i][:, g, :].bitcast(FP8X4),
+                        lhsT_scale=xscl[i][:, g, :],
+                        rhs=base[:, g, 2 * HALF * h : 2 * HALF * (h + 1)].bitcast(FP4X4),
+                        rhs_scale=bsc[:, g, HALF * h : HALF * (h + 1)],
+                        start=(g == 0),
+                        stop=False,
+                    )
+
+            def zout(i, h):
+                a, j = i // 2, i % 2
+                nc.tensor.matmul_mx(
+                    out=z[i, h][:],
+                    lhsT=ocod[a][:, j, :].bitcast(FP8X4),
+                    lhsT_scale=oscl[a][:, j, :],
+                    rhs=wcod[h][:].bitcast(FP8X4),
+                    rhs_scale=wscl[h][:],
+                    start=False,
+                    stop=True,
+                )
+
+            def exp(i, h):
+                if h == 0:
+                    ex[i] = work.tile([P, F], F32, name="ex", tag="ex", bufs=3)
+                nc.scalar.activation(out=ex[i][:, HALF * h : HALF * (h + 1)], in_=z[i, h][:], func=ACT.Exp)
+
+            def mul(i, h):
+                if h == 0:
+                    mass[i] = work.tile([P, GM, 2, P, 2], BF16, name="mass", tag="mass", bufs=4)
+                eng = nc.vector if i == NT - 1 else nc.gpsimd
+                cols = slice(HALF * h, HALF * (h + 1))
+                eng.tensor_tensor(
+                    out=mass[i][:, h],
+                    in0=ex[i][:, cols].rearrange("b (p u e) -> b u p e", u=2, e=2),
+                    in1=spc[:, cols].rearrange("b (p u e) -> b u p e", u=2, e=2),
+                    op=ALU.mult,
+                )
+
+            def mtrans(i):
+                t = psum.tile([P, 2, 2, P], F32, name="xt", tag="xt", bufs=4)
+                mt[i] = t
+                for g in range(GM):
+                    for u in range(2):
+                        nc.tensor.transpose(t[:, u, g, :], mass[i][:, g, u].rearrange("b p e -> b (p e)").bitcast(F32), ident[:])
+
+            def mexit(i):
+                mgrp[i] = work.tile([P, GM * P * 4], BF16, name="mgrp", tag="mgrp", bufs=2, align_bytes=64)
+                nc.vector.tensor_copy(
+                    out=mgrp[i][:].bitcast(F32).rearrange("p (g b u) -> p g b u", g=GM, u=2),
+                    in_=mt[i][:].rearrange("p u g b -> p g b u"),
+                )
+
+            def mquant(i):
+                mcod[i] = work.tile([P, GM, P], U32, name="mcod", tag="mcod", bufs=3, align_bytes=64)
+                mscl[i] = work.tile([P, GM, P], U8, name="mscl", tag="mscl", bufs=3, align_bytes=64)
+                nc.vector.quantize_mx(
+                    out=mcod[i][:].rearrange("p g b -> p (g b)").bitcast(FP8X4),
+                    scales=mscl[i][:].rearrange("p g b -> p (g b)"),
+                    in_=mgrp[i][:],
+                )
+
+            def tmat(i, h):
+                t = psum.tile([P, HALF], F32, name="mm", tag="mm", bufs=4)
+                tg[i, h] = t
+                for g in range(GM):
+                    nc.tensor.matmul_mx(
+                        out=t[:],
+                        lhsT=mcod[i][:, g, :].bitcast(FP8X4),
+                        lhsT_scale=mscl[i][:, g, :],
+                        rhs=proj[:, g, 2 * HALF * h : 2 * HALF * (h + 1)].bitcast(FP4X4),
+                        rhs_scale=psc[:, g, HALF * h : HALF * (h + 1)],
+                        start=(g == 0),
+                        stop=(g == GM - 1),
+                    )
+
+            def tcopy(i, h):
+                if h == 0:
+                    tout[i] = work.tile([P, J], F32, name="tout", tag="tout", bufs=5)
+                cols = slice(HALF * h, HALF * (h + 1))
+                nc.scalar.copy(out=tout[i][:, cols], in_=tg[i, h][:])
+                if i == NT - 1:
+                    nc.sync.dma_start(out=target[P * i : P * (i + 1), cols], in_=tout[i][:, cols])
+                elif h == 1:
+                    nc.sync.dma_start(out=target[P * i : P * (i + 1), :], in_=tout[i][:])
+
+            def lossp(i, h):
+                prods = work.tile([P, HALF], F32, name="prods", tag="prods", bufs=2)
+                nc.vector.scalar_tensor_tensor(
+                    out=prods[:],
+                    in0=tg[i, h][:],
+                    scalar=-1.0 / J,
+                    in1=logs[:, i, HALF * h : HALF * (h + 1)],
+                    op0=ALU.mult,
+                    op1=ALU.mult,
+                    accum_out=acc[h][:, i : i + 1],
+                )
+
+            def ln(i):
+                nc.scalar.activation(out=logs[:, i, :], in_=onl[i // 2][:, i % 2, :], func=ACT.Ln)
+
+            cast(0)
+            xtrans(0, 0)
+            prod(0, 0)
+            xtrans(0, 1)
+            cast(1)
+            prod(0, 1)
+            xtrans(1, 0)
+            prod(1, 0)
+            xquant(0)
+            xtrans(1, 1)
+            prod(1, 1)
+            ln(0)
+            ln(1)
+            cast(2)
+            wgroup(0)
+            wgroup(1)
+            zrest(0, 0)
+            zrest(0, 1)
+            xtrans(2, 0)
+            prod(2, 0)
+            xquant(1)
+            xtrans(2, 1)
+            prod(2, 1)
+            ln(2)
+            ln(3)
+            otrans(0)
+            oexit(0)
+            xquant(2)
+            cast(3)
+            zrest(1, 0)
+            zrest(1, 1)
+            xtrans(3, 0)
+            oquant(0)
+            prod(3, 0)
+            xtrans(3, 1)
+            wquant(0)
+            prod(3, 1)
+            wquant(1)
+            ln(4)
+            ln(5)
+            cast(4)
+            zout(0, 0)
+            zout(0, 1)
+            zout(1, 0)
+            zout(1, 1)
+            xtrans(4, 0)
+            prod(4, 0)
+            xquant(3)
+            xtrans(4, 1)
+            prod(4, 1)
+            ln(6)
+            ln(7)
+            exp(0, 0)
+            mul(0, 0)
+            exp(0, 1)
+            mul(0, 1)
+            exp(1, 0)
+            mul(1, 0)
+            exp(1, 1)
+            mul(1, 1)
+            otrans(1)
+            oexit(1)
+            xquant(4)
+            cast(5)
+            xtrans(5, 0)
+            prod(5, 0)
+            xtrans(5, 1)
+            prod(5, 1)
+            cast(6)
+            oquant(1)
+            mtrans(0)
+            mexit(0)
+            xquant(5)
+            mquant(0)
+            zrest(2, 0)
+            zout(2, 0)
+            exp(2, 0)
+            mul(2, 0)
+            zrest(2, 1)
+            zout(2, 1)
+            exp(2, 1)
+            mul(2, 1)
+            xtrans(6, 0)
+            prod(6, 0)
+            xtrans(6, 1)
+            prod(6, 1)
+            cast(7)
+            otrans(2)
+            oexit(2)
+            mtrans(1)
+            mexit(1)
+            xquant(6)
+            oquant(2)
+            mquant(1)
+            zrest(3, 0)
+            zout(3, 0)
+            exp(3, 0)
+            mul(3, 0)
+            zrest(3, 1)
+            zout(3, 1)
+            exp(3, 1)
+            mul(3, 1)
+            tmat(0, 0)
+            tmat(0, 1)
+            tcopy(0, 0)
+            lossp(0, 0)
+            tcopy(0, 1)
+            lossp(0, 1)
+            xtrans(7, 0)
+            prod(7, 0)
+            xtrans(7, 1)
+            prod(7, 1)
+            mtrans(2)
+            mexit(2)
+            xquant(7)
+            mquant(2)
+            zrest(4, 0)
+            zout(4, 0)
+            exp(4, 0)
+            mul(4, 0)
+            zrest(4, 1)
+            zout(4, 1)
+            exp(4, 1)
+            mul(4, 1)
+            tmat(1, 0)
+            tmat(1, 1)
+            tcopy(1, 0)
+            lossp(1, 0)
+            tcopy(1, 1)
+            lossp(1, 1)
+            otrans(3)
+            oexit(3)
+            mtrans(3)
+            mexit(3)
+            oquant(3)
+            mquant(3)
+            zrest(5, 0)
+            zout(5, 0)
+            exp(5, 0)
+            mul(5, 0)
+            zrest(5, 1)
+            zout(5, 1)
+            exp(5, 1)
+            mul(5, 1)
+            tmat(2, 0)
+            tmat(2, 1)
+            tcopy(2, 0)
+            lossp(2, 0)
+            tcopy(2, 1)
+            lossp(2, 1)
+            mtrans(4)
+            mexit(4)
+            mquant(4)
+            zrest(6, 0)
+            zout(6, 0)
+            exp(6, 0)
+            mul(6, 0)
+            zrest(6, 1)
+            zout(6, 1)
+            exp(6, 1)
+            mul(6, 1)
+            tmat(3, 0)
+            tmat(3, 1)
+            tcopy(3, 0)
+            lossp(3, 0)
+            tcopy(3, 1)
+            lossp(3, 1)
+            mtrans(5)
+            mexit(5)
+            mquant(5)
+            zrest(7, 0)
+            zout(7, 0)
+            exp(7, 0)
+            mul(7, 0)
+            zrest(7, 1)
+            zout(7, 1)
+            exp(7, 1)
+            mul(7, 1)
+            tmat(4, 0)
+            tmat(4, 1)
+            tcopy(4, 0)
+            lossp(4, 0)
+            tcopy(4, 1)
+            lossp(4, 1)
+            mtrans(6)
+            mexit(6)
+            mquant(6)
+            tmat(5, 0)
+            tmat(5, 1)
+            tcopy(5, 0)
+            lossp(5, 0)
+            tcopy(5, 1)
+            lossp(5, 1)
+            mtrans(7)
+            mexit(7)
+            mquant(7)
+            tmat(6, 0)
+            tmat(6, 1)
+            tcopy(6, 0)
+            lossp(6, 0)
+            tcopy(6, 1)
+            lossp(6, 1)
+            tmat(7, 0)
+            tmat(7, 1)
+            tcopy(7, 0)
+            lossp(7, 0)
+            tcopy(7, 1)
+            lossp(7, 1)
+            nc.vector.tensor_tensor(out=lpad[:, 0:NT], in0=acc[0][:], in1=acc[1][:], op=ALU.add)
+            lt = psum.tile([P, 2, 2, P], F32, name="xt", tag="xt", bufs=4)
+            nc.tensor.transpose(lt[:, 0, 0, :], lpad[:], ident[:])
+            nc.scalar.copy(out=lrow[:], in_=lt[0:32, 0, 0, :])
+            nc.sync.dma_start(out=loss.rearrange("(i b) -> i b", b=P), in_=lrow[0:NT, :])

@@ -61,7 +61,7 @@ def tile_c51_shifted_log_loss_s3_kernel(
         ocod = [kept([P, 2, P], U32, "ocod%d" % i) for i in range(NT // 2)]
         oscl = [kept([P, 2, P], U8, "oscl%d" % i) for i in range(NT // 2)]
 
-        if True:
+        with tc.manual_schedule():
             nc.vector.memset(one[:], 1.0)
             nc.vector.memset(bsc[:].rearrange("p g n -> p (g n)").bitcast(I32), 0)
             nc.vector.memset(psc[:].rearrange("p g n -> p (g n)").bitcast(I32), 0)
@@ -70,6 +70,10 @@ def tile_c51_shifted_log_loss_s3_kernel(
             make_identity(nc, ident[:])
 
             def load_x(i):
+                if i == 0:
+                    nc.sync.dma_start(out=xr[i][:, 0:1024], in_=x_rest_bytes[0:P, 0:1024])
+                    nc.sync.dma_start(out=xr[i][:, 1024:2048], in_=x_rest_bytes[0:P, 1024:2048])
+                    return
                 nc.sync.dma_start(out=xr[i][:], in_=x_rest_bytes[P * i : P * (i + 1), :])
 
             def load_onl(a):
@@ -79,7 +83,7 @@ def tile_c51_shifted_log_loss_s3_kernel(
                 nc.sync.dma_start(out=xo[a][:], in_=x_out[2 * P * a : 2 * P * (a + 1), :].rearrange("(i r) k -> r i k", r=P))
 
             load_x(0)
-            nc.sync.dma_start(out=sc[:].rearrange("p g u e -> p g (u e)"), in_=x_rest_scale.rearrange("o (g p t) -> p (o g) t", p=P, t=4))
+            load_x(2)
             load_x(1)
             load_onl(0)
             for q in range(4):
@@ -87,28 +91,28 @@ def tile_c51_shifted_log_loss_s3_kernel(
                     out=bsc[32 * q : 32 * q + 4].bitcast(I32),
                     in_=base_scales[:, 4 * q : 4 * q + 4, :].rearrange("g r n -> r g n").bitcast(I32),
                 )
-            nc.sync.dma_start(out=base[:], in_=base_words.rearrange("g p n -> p g n"))
-            load_x(2)
-            load_onl(1)
+            nc.sync.dma_start(out=sc[:].rearrange("p g u e -> p g (u e)"), in_=x_rest_scale.rearrange("o (g p t) -> p (o g) t", p=P, t=4))
             nc.sync.dma_start(out=wraw[:], in_=w_out.rearrange("(p j) n -> p j n", j=4))
-            load_x(3)
-            load_xo(0)
-            load_onl(2)
-            load_onl(3)
-            load_x(4)
+            load_onl(1)
             for q in range(4):
                 nc.sync.dma_start(
                     out=psc[32 * q : 32 * q + 4].bitcast(I32),
                     in_=proj_scales[:, 4 * q : 4 * q + 4, :].rearrange("g r n -> r g n").bitcast(I32),
                 )
+            load_x(3)
+            load_onl(2)
+            nc.sync.dma_start(out=base[:], in_=base_words.rearrange("g p n -> p g n"))
+            load_onl(3)
+            nc.sync.dma_start(out=proj[:], in_=proj_words.rearrange("g p n -> p g n"))
+            load_x(7)
+            load_xo(0)
+            load_x(4)
+            load_xo(3)
             nc.sync.dma_start(out=spc[:], in_=spacing.partition_broadcast(P))
             load_xo(1)
-            load_x(5)
-            nc.sync.dma_start(out=proj[:], in_=proj_words.rearrange("g p n -> p g n"))
             load_x(6)
+            load_x(5)
             load_xo(2)
-            load_x(7)
-            load_xo(3)
 
             wide = {}
             xt = {}
@@ -126,9 +130,12 @@ def tile_c51_shifted_log_loss_s3_kernel(
             def cast(i):
                 t = work.tile([P, KR], BF16, name="wide", tag="wide", bufs=4)
                 wide[i] = t
-                if i < 2:
-                    nc.scalar.copy(out=t[:, 0:512], in_=xr[i][:, 0:512].bitcast(FP8))
-                    nc.vector.tensor_copy(out=t[:, 512:1024], in_=xr[i][:, 512:1024].bitcast(FP8))
+                if i == 0:
+                    for c in (0, 1024):
+                        nc.scalar.copy(out=t[:, c : c + 512], in_=xr[i][:, c : c + 512].bitcast(FP8))
+                        nc.vector.tensor_copy(out=t[:, c + 512 : c + 1024], in_=xr[i][:, c + 512 : c + 1024].bitcast(FP8))
+                elif i == 1:
+                    nc.scalar.copy(out=t[:, 0:1024], in_=xr[i][:, 0:1024].bitcast(FP8))
                     nc.vector.tensor_copy(out=t[:, 1024:2048], in_=xr[i][:, 1024:2048].bitcast(FP8))
                 else:
                     nc.scalar.copy(out=t[:], in_=xr[i][:].bitcast(FP8))
@@ -143,7 +150,7 @@ def tile_c51_shifted_log_loss_s3_kernel(
                         nc.tensor.transpose(t[:, u, gg, :], words[:, 256 * g + u : 256 * (g + 1) : 2], ident[:])
 
             def prod(i, b):
-                if b == 0:
+                if i not in grp:
                     grp[i] = work.tile([P, GR, P, 2, 2], BF16, name="grp", tag="grp", bufs=4, align_bytes=64)
                 t = xt[i, b][:].rearrange("p u g r -> p (u g r)").bitcast(BF16).rearrange("p (u g r e) -> p g r u e", u=2, g=2, e=2)
                 s = sc[:, 2 * b : 2 * b + 2].unsqueeze(2).to_broadcast([P, 2, P, 2, 2])
@@ -166,7 +173,7 @@ def tile_c51_shifted_log_loss_s3_kernel(
 
             def oexit(a):
                 grp["o", a] = work.tile([P, 2 * P * 4], BF16, name="ogrp", tag="ogrp", bufs=2, align_bytes=64)
-                nc.vector.tensor_copy(
+                nc.scalar.copy(
                     out=grp["o", a][:].bitcast(F32).rearrange("p (i r u) -> p i r u", i=2, u=2),
                     in_=xt["o", a][:].rearrange("p u i r -> p i r u"),
                 )
@@ -218,14 +225,14 @@ def tile_c51_shifted_log_loss_s3_kernel(
                 )
 
             def exp(i, h):
-                if h == 0:
+                if i not in ex:
                     ex[i] = work.tile([P, F], F32, name="ex", tag="ex", bufs=3)
                 nc.scalar.activation(out=ex[i][:, HALF * h : HALF * (h + 1)], in_=z[i, h][:], func=ACT.Exp)
 
             def mul(i, h):
-                if h == 0:
+                if i not in mass:
                     mass[i] = work.tile([P, GM, 2, P, 2], BF16, name="mass", tag="mass", bufs=4)
-                eng = nc.vector if i == NT - 1 else nc.gpsimd
+                eng = nc.vector
                 cols = slice(HALF * h, HALF * (h + 1))
                 eng.tensor_tensor(
                     out=mass[i][:, h],
@@ -243,7 +250,7 @@ def tile_c51_shifted_log_loss_s3_kernel(
 
             def mexit(i):
                 mgrp[i] = work.tile([P, GM * P * 4], BF16, name="mgrp", tag="mgrp", bufs=2, align_bytes=64)
-                nc.vector.tensor_copy(
+                nc.scalar.copy(
                     out=mgrp[i][:].bitcast(F32).rearrange("p (g b u) -> p g b u", g=GM, u=2),
                     in_=mt[i][:].rearrange("p u g b -> p g b u"),
                 )
@@ -272,14 +279,11 @@ def tile_c51_shifted_log_loss_s3_kernel(
                     )
 
             def tcopy(i, h):
-                if h == 0:
+                if i not in tout:
                     tout[i] = work.tile([P, J], F32, name="tout", tag="tout", bufs=5)
                 cols = slice(HALF * h, HALF * (h + 1))
                 nc.scalar.copy(out=tout[i][:, cols], in_=tg[i, h][:])
-                if i == NT - 1:
-                    nc.sync.dma_start(out=target[P * i : P * (i + 1), cols], in_=tout[i][:, cols])
-                elif h == 1:
-                    nc.sync.dma_start(out=target[P * i : P * (i + 1), :], in_=tout[i][:])
+                nc.sync.dma_start(out=target[P * i : P * (i + 1), cols], in_=tout[i][:, cols])
 
             def lossp(i, h):
                 prods = work.tile([P, HALF], F32, name="prods", tag="prods", bufs=2)
@@ -297,213 +301,213 @@ def tile_c51_shifted_log_loss_s3_kernel(
                 nc.scalar.activation(out=logs[:, i, :], in_=onl[i // 2][:, i % 2, :], func=ACT.Ln)
 
             cast(0)
-            xtrans(0, 0)
-            prod(0, 0)
-            xtrans(0, 1)
             cast(1)
-            prod(0, 1)
-            xtrans(1, 0)
-            prod(1, 0)
-            xquant(0)
-            xtrans(1, 1)
-            prod(1, 1)
+            xtrans(0, 0)
+            xtrans(0, 1)
+            prod(0, 0)
             ln(0)
-            ln(1)
+            xtrans(1, 1)
+            xtrans(1, 0)
+            prod(0, 1)
             cast(2)
             wgroup(0)
-            wgroup(1)
-            zrest(0, 0)
-            zrest(0, 1)
-            xtrans(2, 0)
-            prod(2, 0)
-            xquant(1)
+            prod(1, 1)
+            ln(1)
             xtrans(2, 1)
+            xtrans(2, 0)
             prod(2, 1)
-            ln(2)
             ln(3)
-            otrans(0)
-            oexit(0)
-            xquant(2)
+            xquant(0)
+            ln(2)
+            wgroup(1)
+            prod(1, 0)
             cast(3)
-            zrest(1, 0)
-            zrest(1, 1)
-            xtrans(3, 0)
-            oquant(0)
-            prod(3, 0)
-            xtrans(3, 1)
             wquant(0)
-            prod(3, 1)
-            wquant(1)
             ln(4)
+            xquant(1)
+            xtrans(3, 0)
+            zrest(0, 0)
+            prod(2, 0)
             ln(5)
-            cast(4)
-            zout(0, 0)
-            zout(0, 1)
-            zout(1, 0)
-            zout(1, 1)
-            xtrans(4, 0)
-            prod(4, 0)
-            xquant(3)
-            xtrans(4, 1)
-            prod(4, 1)
-            ln(6)
+            zrest(0, 1)
+            prod(3, 0)
             ln(7)
-            exp(0, 0)
-            mul(0, 0)
-            exp(0, 1)
-            mul(0, 1)
-            exp(1, 0)
-            mul(1, 0)
-            exp(1, 1)
-            mul(1, 1)
-            otrans(1)
-            oexit(1)
-            xquant(4)
-            cast(5)
-            xtrans(5, 0)
-            prod(5, 0)
-            xtrans(5, 1)
-            prod(5, 1)
-            cast(6)
-            oquant(1)
-            mtrans(0)
-            mexit(0)
-            xquant(5)
-            mquant(0)
-            zrest(2, 0)
-            zout(2, 0)
-            exp(2, 0)
-            mul(2, 0)
-            zrest(2, 1)
-            zout(2, 1)
-            exp(2, 1)
-            mul(2, 1)
-            xtrans(6, 0)
-            prod(6, 0)
-            xtrans(6, 1)
-            prod(6, 1)
+            zrest(1, 1)
+            xquant(2)
+            ln(6)
+            wquant(1)
+            otrans(0)
+            cast(4)
+            xtrans(3, 1)
+            zrest(1, 0)
+            prod(3, 1)
+            oexit(0)
             cast(7)
+            xtrans(4, 0)
+            oquant(0)
+            xtrans(4, 1)
+            xquant(3)
+            zout(0, 1)
+            cast(5)
+            prod(4, 0)
+            zout(1, 0)
+            zout(0, 0)
+            otrans(1)
+            exp(0, 0)
+            prod(4, 1)
+            xtrans(5, 1)
+            xtrans(5, 0)
+            prod(5, 1)
+            zout(1, 1)
             otrans(2)
-            oexit(2)
-            mtrans(1)
-            mexit(1)
-            xquant(6)
-            oquant(2)
-            mquant(1)
+            exp(0, 1)
+            prod(5, 0)
             zrest(3, 0)
-            zout(3, 0)
-            exp(3, 0)
-            mul(3, 0)
+            exp(1, 0)
+            exp(1, 1)
+            mul(0, 1)
+            zrest(2, 0)
+            cast(6)
+            mul(1, 0)
+            zrest(2, 1)
+            mul(1, 1)
+            oexit(1)
+            mul(0, 0)
+            oexit(2)
             zrest(3, 1)
+            xquant(4)
+            oquant(2)
+            xquant(5)
+            xtrans(6, 1)
+            mtrans(0)
+            oquant(1)
+            xtrans(6, 0)
+            prod(6, 1)
+            mexit(0)
+            zout(2, 1)
             zout(3, 1)
-            exp(3, 1)
-            mul(3, 1)
-            tmat(0, 0)
-            tmat(0, 1)
-            tcopy(0, 0)
-            lossp(0, 0)
-            tcopy(0, 1)
-            lossp(0, 1)
+            exp(2, 1)
+            zout(2, 0)
+            prod(6, 0)
             xtrans(7, 0)
-            prod(7, 0)
+            exp(3, 1)
+            zout(3, 0)
+            mtrans(1)
+            exp(2, 0)
+            mul(2, 1)
             xtrans(7, 1)
-            prod(7, 1)
-            mtrans(2)
-            mexit(2)
-            xquant(7)
-            mquant(2)
-            zrest(4, 0)
-            zout(4, 0)
-            exp(4, 0)
-            mul(4, 0)
-            zrest(4, 1)
-            zout(4, 1)
-            exp(4, 1)
-            mul(4, 1)
-            tmat(1, 0)
-            tmat(1, 1)
-            tcopy(1, 0)
-            lossp(1, 0)
-            tcopy(1, 1)
-            lossp(1, 1)
+            exp(3, 0)
+            mquant(0)
             otrans(3)
+            mul(2, 0)
+            mexit(1)
+            tmat(0, 0)
+            mul(3, 0)
             oexit(3)
+            tmat(0, 1)
+            mquant(1)
+            tcopy(0, 0)
+            zrest(4, 0)
+            mul(3, 1)
+            tcopy(0, 1)
+            prod(7, 0)
+            tmat(1, 1)
+            zout(4, 0)
+            xquant(6)
+            tcopy(1, 1)
             mtrans(3)
+            mtrans(2)
+            lossp(0, 0)
+            exp(4, 0)
+            lossp(0, 1)
+            mexit(2)
+            zrest(4, 1)
             mexit(3)
-            oquant(3)
-            mquant(3)
+            mul(4, 0)
+            zout(4, 1)
+            mquant(2)
+            tmat(1, 0)
+            lossp(1, 1)
+            exp(4, 1)
             zrest(5, 0)
+            tcopy(1, 0)
+            prod(7, 1)
             zout(5, 0)
-            exp(5, 0)
-            mul(5, 0)
             zrest(5, 1)
+            mul(4, 1)
+            exp(5, 0)
+            xquant(7)
             zout(5, 1)
-            exp(5, 1)
-            mul(5, 1)
-            tmat(2, 0)
-            tmat(2, 1)
-            tcopy(2, 0)
-            lossp(2, 0)
-            tcopy(2, 1)
-            lossp(2, 1)
+            lossp(1, 0)
             mtrans(4)
-            mexit(4)
-            mquant(4)
-            zrest(6, 0)
-            zout(6, 0)
-            exp(6, 0)
-            mul(6, 0)
+            exp(5, 1)
             zrest(6, 1)
-            zout(6, 1)
-            exp(6, 1)
-            mul(6, 1)
-            tmat(3, 0)
+            mul(5, 0)
+            mexit(4)
+            mquant(3)
+            tmat(2, 1)
+            oquant(3)
+            mquant(4)
             tmat(3, 1)
-            tcopy(3, 0)
-            lossp(3, 0)
-            tcopy(3, 1)
+            mul(5, 1)
+            tcopy(2, 1)
+            zout(6, 1)
             lossp(3, 1)
+            tmat(2, 0)
+            exp(6, 1)
             mtrans(5)
+            lossp(2, 1)
+            tcopy(2, 0)
+            zrest(6, 0)
+            tcopy(3, 1)
+            mul(6, 1)
             mexit(5)
-            mquant(5)
+            lossp(2, 0)
+            zout(6, 0)
             zrest(7, 0)
+            exp(6, 0)
+            mquant(5)
+            mul(6, 0)
+            tmat(3, 0)
             zout(7, 0)
-            exp(7, 0)
-            mul(7, 0)
-            zrest(7, 1)
-            zout(7, 1)
-            exp(7, 1)
-            mul(7, 1)
+            lossp(3, 0)
             tmat(4, 0)
-            tmat(4, 1)
-            tcopy(4, 0)
+            exp(7, 0)
+            zrest(7, 1)
             lossp(4, 0)
-            tcopy(4, 1)
-            lossp(4, 1)
+            tcopy(3, 0)
+            mul(7, 0)
+            zout(7, 1)
+            tcopy(4, 0)
             mtrans(6)
-            mexit(6)
-            mquant(6)
-            tmat(5, 0)
+            exp(7, 1)
             tmat(5, 1)
-            tcopy(5, 0)
-            lossp(5, 0)
+            tmat(5, 0)
+            mexit(6)
+            mul(7, 1)
+            tmat(4, 1)
             tcopy(5, 1)
-            lossp(5, 1)
+            mquant(6)
+            lossp(5, 0)
             mtrans(7)
-            mexit(7)
-            mquant(7)
-            tmat(6, 0)
+            tcopy(4, 1)
             tmat(6, 1)
-            tcopy(6, 0)
-            lossp(6, 0)
+            lossp(5, 1)
+            mexit(7)
+            tcopy(5, 0)
+            lossp(4, 1)
+            tmat(6, 0)
             tcopy(6, 1)
-            lossp(6, 1)
-            tmat(7, 0)
+            mquant(7)
+            lossp(6, 0)
             tmat(7, 1)
-            tcopy(7, 0)
-            lossp(7, 0)
+            tmat(7, 0)
+            lossp(6, 1)
+            tcopy(6, 0)
             tcopy(7, 1)
+            lossp(7, 0)
             lossp(7, 1)
+            tcopy(7, 0)
             nc.vector.tensor_tensor(out=lpad[:, 0:NT], in0=acc[0][:], in1=acc[1][:], op=ALU.add)
             lt = psum.tile([P, 2, 2, P], F32, name="xt", tag="xt", bufs=4)
             nc.tensor.transpose(lt[:, 0, 0, :], lpad[:], ident[:])

@@ -39,6 +39,7 @@ def tile_c51_shifted_log_loss_s3_kernel(
         xr = [kept([P, KR], U8, "xr%d" % i) for i in range(NT)]
         sc = kept([P, GR, 2, 2], F32, "sc")
         base = kept([P, GR, 2 * F], U8, "base")
+        scb = kept([P, KR], F32, "scb")
         bsc = kept([P, GR, F], U8, "bsc")
         proj = kept([P, GM, 2 * J], U8, "proj")
         psc = kept([P, GM, J], U8, "psc")
@@ -83,36 +84,37 @@ def tile_c51_shifted_log_loss_s3_kernel(
                 nc.sync.dma_start(out=xo[a][:], in_=x_out[2 * P * a : 2 * P * (a + 1), :].rearrange("(i r) k -> r i k", r=P))
 
             load_x(0)
+            load_xo(0)
             load_x(2)
+            nc.sync.dma_start(out=sc[:].rearrange("p g u e -> p g (u e)"), in_=x_rest_scale.rearrange("o (g p t) -> p (o g) t", p=P, t=4))
             load_x(1)
+            nc.sync.dma_start(out=wraw[:], in_=w_out.rearrange("(p j) n -> p j n", j=4))
             load_onl(0)
+            load_xo(1)
+            load_onl(1)
+            nc.sync.dma_start(out=base[:], in_=base_words.rearrange("g p n -> p g n"))
             for q in range(4):
                 nc.sync.dma_start(
                     out=bsc[32 * q : 32 * q + 4].bitcast(I32),
                     in_=base_scales[:, 4 * q : 4 * q + 4, :].rearrange("g r n -> r g n").bitcast(I32),
                 )
-            nc.sync.dma_start(out=sc[:].rearrange("p g u e -> p g (u e)"), in_=x_rest_scale.rearrange("o (g p t) -> p (o g) t", p=P, t=4))
-            nc.sync.dma_start(out=wraw[:], in_=w_out.rearrange("(p j) n -> p j n", j=4))
-            load_onl(1)
+            load_onl(2)
+            load_x(3)
+            nc.sync.dma_start(out=spc[:], in_=spacing.partition_broadcast(P))
+            nc.sync.dma_start(out=scb[:], in_=x_rest_scale.rearrange("o k -> (o k)").partition_broadcast(P))
+            load_x(5)
+            load_x(4)
+            load_xo(2)
+            load_onl(3)
+            load_x(7)
+            load_xo(3)
+            nc.sync.dma_start(out=proj[:], in_=proj_words.rearrange("g p n -> p g n"))
+            load_x(6)
             for q in range(4):
                 nc.sync.dma_start(
                     out=psc[32 * q : 32 * q + 4].bitcast(I32),
                     in_=proj_scales[:, 4 * q : 4 * q + 4, :].rearrange("g r n -> r g n").bitcast(I32),
                 )
-            load_x(3)
-            load_onl(2)
-            nc.sync.dma_start(out=base[:], in_=base_words.rearrange("g p n -> p g n"))
-            load_onl(3)
-            nc.sync.dma_start(out=proj[:], in_=proj_words.rearrange("g p n -> p g n"))
-            load_x(7)
-            load_xo(0)
-            load_x(4)
-            load_xo(3)
-            nc.sync.dma_start(out=spc[:], in_=spacing.partition_broadcast(P))
-            load_xo(1)
-            load_x(6)
-            load_x(5)
-            load_xo(2)
 
             wide = {}
             xt = {}
@@ -128,6 +130,11 @@ def tile_c51_shifted_log_loss_s3_kernel(
             tout = {}
 
             def cast(i):
+                if i in (3, 4, 5, 6, 7,):
+                    t = work.tile([P, KR], BF16, name="wide", tag="wide", bufs=4)
+                    wide[i] = t
+                    nc.vector.tensor_tensor(out=t[:], in0=xr[i][:].bitcast(FP8), in1=scb[:], op=ALU.mult)
+                    return
                 t = work.tile([P, KR], BF16, name="wide", tag="wide", bufs=4)
                 wide[i] = t
                 if i == 0:
@@ -152,6 +159,12 @@ def tile_c51_shifted_log_loss_s3_kernel(
             def prod(i, b):
                 if i not in grp:
                     grp[i] = work.tile([P, GR, P, 2, 2], BF16, name="grp", tag="grp", bufs=4, align_bytes=64)
+                if i in (3, 4, 5, 6, 7,):
+                    nc.scalar.copy(
+                        out=grp[i][:, 2 * b : 2 * b + 2].rearrange("p g r u e -> p (g r u e)").bitcast(F32).rearrange("p (g r u) -> p g r u", g=2, u=2),
+                        in_=xt[i, b][:].rearrange("p u g r -> p g r u"),
+                    )
+                    return
                 t = xt[i, b][:].rearrange("p u g r -> p (u g r)").bitcast(BF16).rearrange("p (u g r e) -> p g r u e", u=2, g=2, e=2)
                 s = sc[:, 2 * b : 2 * b + 2].unsqueeze(2).to_broadcast([P, 2, P, 2, 2])
                 nc.vector.tensor_tensor(out=grp[i][:, 2 * b : 2 * b + 2], in0=t, in1=s, op=ALU.mult)
@@ -231,15 +244,16 @@ def tile_c51_shifted_log_loss_s3_kernel(
 
             def mul(i, h):
                 if i not in mass:
-                    mass[i] = work.tile([P, GM, 2, P, 2], BF16, name="mass", tag="mass", bufs=4)
-                eng = nc.vector
+                    mass[i] = work.tile([P, GM, 2, P, 2], BF16, name="mass", tag="mass", bufs=3)
                 cols = slice(HALF * h, HALF * (h + 1))
-                eng.tensor_tensor(
-                    out=mass[i][:, h],
-                    in0=ex[i][:, cols].rearrange("b (p u e) -> b u p e", u=2, e=2),
-                    in1=spc[:, cols].rearrange("b (p u e) -> b u p e", u=2, e=2),
-                    op=ALU.mult,
-                )
+                dst = mass[i][:, h]
+                src = ex[i][:, cols].rearrange("b (p u e) -> b u p e", u=2, e=2)
+                fac = spc[:, cols].rearrange("b (p u e) -> b u p e", u=2, e=2)
+                if i >= 5:
+                    nc.vector.tensor_tensor(out=dst, in0=src, in1=fac, op=ALU.mult)
+                else:
+                    for u in range(2):
+                        nc.gpsimd.tensor_tensor(out=dst[:, u], in0=src[:, u], in1=fac[:, u], op=ALU.mult)
 
             def mtrans(i):
                 t = psum.tile([P, 2, 2, P], F32, name="xt", tag="xt", bufs=4)
@@ -279,11 +293,9 @@ def tile_c51_shifted_log_loss_s3_kernel(
                     )
 
             def tcopy(i, h):
-                if i not in tout:
-                    tout[i] = work.tile([P, J], F32, name="tout", tag="tout", bufs=5)
-                cols = slice(HALF * h, HALF * (h + 1))
-                nc.scalar.copy(out=tout[i][:, cols], in_=tg[i, h][:])
-                nc.sync.dma_start(out=target[P * i : P * (i + 1), cols], in_=tout[i][:, cols])
+                half = work.tile([P, HALF], F32, name="tout", tag="tout", bufs=8)
+                nc.scalar.copy(out=half[:], in_=tg[i, h][:])
+                nc.sync.dma_start(out=target[P * i : P * (i + 1), HALF * h : HALF * (h + 1)], in_=half[:])
 
             def lossp(i, h):
                 prods = work.tile([P, HALF], F32, name="prods", tag="prods", bufs=2)
@@ -300,214 +312,214 @@ def tile_c51_shifted_log_loss_s3_kernel(
             def ln(i):
                 nc.scalar.activation(out=logs[:, i, :], in_=onl[i // 2][:, i % 2, :], func=ACT.Ln)
 
+            otrans(0)
             cast(0)
-            cast(1)
             xtrans(0, 0)
-            xtrans(0, 1)
+            cast(1)
             prod(0, 0)
+            cast(2)
+            xtrans(0, 1)
+            oexit(0)
+            xtrans(1, 0)
             ln(0)
             xtrans(1, 1)
-            xtrans(1, 0)
-            prod(0, 1)
-            cast(2)
-            wgroup(0)
-            prod(1, 1)
             ln(1)
-            xtrans(2, 1)
-            xtrans(2, 0)
-            prod(2, 1)
-            ln(3)
-            xquant(0)
-            ln(2)
-            wgroup(1)
+            otrans(1)
+            prod(0, 1)
             prod(1, 0)
-            cast(3)
-            wquant(0)
-            ln(4)
+            prod(1, 1)
+            xtrans(2, 0)
+            oexit(1)
+            xtrans(2, 1)
+            xquant(0)
+            wgroup(0)
             xquant(1)
-            xtrans(3, 0)
+            ln(2)
             zrest(0, 0)
             prod(2, 0)
-            ln(5)
-            zrest(0, 1)
-            prod(3, 0)
-            ln(7)
-            zrest(1, 1)
-            xquant(2)
-            ln(6)
-            wquant(1)
-            otrans(0)
-            cast(4)
-            xtrans(3, 1)
-            zrest(1, 0)
-            prod(3, 1)
-            oexit(0)
-            cast(7)
-            xtrans(4, 0)
             oquant(0)
-            xtrans(4, 1)
-            xquant(3)
-            zout(0, 1)
-            cast(5)
-            prod(4, 0)
-            zout(1, 0)
+            wquant(0)
+            ln(3)
+            prod(2, 1)
+            wgroup(1)
+            wquant(1)
+            xquant(2)
+            zrest(0, 1)
+            oquant(1)
             zout(0, 0)
-            otrans(1)
+            cast(3)
+            ln(4)
+            ln(5)
+            zrest(1, 0)
+            zout(0, 1)
+            cast(4)
+            zrest(1, 1)
             exp(0, 0)
-            prod(4, 1)
-            xtrans(5, 1)
-            xtrans(5, 0)
-            prod(5, 1)
-            zout(1, 1)
-            otrans(2)
             exp(0, 1)
-            prod(5, 0)
-            zrest(3, 0)
+            zout(1, 0)
+            zout(1, 1)
             exp(1, 0)
             exp(1, 1)
-            mul(0, 1)
             zrest(2, 0)
-            cast(6)
-            mul(1, 0)
-            zrest(2, 1)
-            mul(1, 1)
-            oexit(1)
-            mul(0, 0)
-            oexit(2)
-            zrest(3, 1)
-            xquant(4)
-            oquant(2)
-            xquant(5)
-            xtrans(6, 1)
-            mtrans(0)
-            oquant(1)
-            xtrans(6, 0)
-            prod(6, 1)
-            mexit(0)
-            zout(2, 1)
-            zout(3, 1)
-            exp(2, 1)
             zout(2, 0)
-            prod(6, 0)
-            xtrans(7, 0)
-            exp(3, 1)
-            zout(3, 0)
-            mtrans(1)
-            exp(2, 0)
-            mul(2, 1)
-            xtrans(7, 1)
-            exp(3, 0)
-            mquant(0)
+            ln(6)
+            zrest(2, 1)
+            mul(0, 0)
+            mul(0, 1)
+            otrans(2)
+            xtrans(3, 0)
+            mul(1, 0)
+            zout(2, 1)
+            cast(5)
+            xtrans(3, 1)
+            oexit(2)
+            xtrans(4, 0)
+            prod(3, 0)
+            prod(3, 1)
+            xtrans(4, 1)
+            prod(4, 0)
             otrans(3)
-            mul(2, 0)
-            mexit(1)
-            tmat(0, 0)
-            mul(3, 0)
+            xtrans(5, 0)
+            mul(1, 1)
+            xquant(3)
+            xtrans(5, 1)
+            prod(4, 1)
+            ln(7)
+            mtrans(0)
+            zrest(3, 0)
+            zrest(3, 1)
+            exp(2, 0)
+            exp(2, 1)
+            zout(3, 0)
+            mexit(0)
+            zout(3, 1)
+            cast(6)
+            exp(3, 0)
             oexit(3)
-            tmat(0, 1)
-            mquant(1)
-            tcopy(0, 0)
+            xquant(4)
+            mquant(0)
+            exp(3, 1)
             zrest(4, 0)
-            mul(3, 1)
-            tcopy(0, 1)
-            prod(7, 0)
-            tmat(1, 1)
-            zout(4, 0)
-            xquant(6)
-            tcopy(1, 1)
-            mtrans(3)
-            mtrans(2)
-            lossp(0, 0)
-            exp(4, 0)
-            lossp(0, 1)
-            mexit(2)
             zrest(4, 1)
-            mexit(3)
-            mul(4, 0)
+            mul(2, 0)
+            mul(2, 1)
+            tmat(0, 0)
+            oquant(2)
+            zout(4, 0)
+            mul(3, 0)
+            prod(5, 0)
+            tmat(0, 1)
+            xtrans(6, 0)
+            tcopy(0, 0)
+            lossp(0, 0)
+            mtrans(1)
+            mul(3, 1)
+            prod(5, 1)
+            xquant(5)
+            exp(4, 0)
+            mexit(1)
+            mtrans(2)
+            xtrans(6, 1)
             zout(4, 1)
-            mquant(2)
-            tmat(1, 0)
-            lossp(1, 1)
-            exp(4, 1)
+            mquant(1)
+            prod(6, 0)
+            lossp(0, 1)
             zrest(5, 0)
-            tcopy(1, 0)
-            prod(7, 1)
-            zout(5, 0)
-            zrest(5, 1)
-            mul(4, 1)
-            exp(5, 0)
-            xquant(7)
-            zout(5, 1)
-            lossp(1, 0)
-            mtrans(4)
-            exp(5, 1)
-            zrest(6, 1)
-            mul(5, 0)
-            mexit(4)
-            mquant(3)
-            tmat(2, 1)
+            exp(4, 1)
             oquant(3)
-            mquant(4)
-            tmat(3, 1)
-            mul(5, 1)
-            tcopy(2, 1)
-            zout(6, 1)
-            lossp(3, 1)
-            tmat(2, 0)
-            exp(6, 1)
-            mtrans(5)
-            lossp(2, 1)
-            tcopy(2, 0)
+            prod(6, 1)
+            cast(7)
+            tcopy(0, 1)
+            mexit(2)
+            zrest(5, 1)
+            tmat(1, 0)
+            zout(5, 0)
+            zout(5, 1)
+            tcopy(1, 0)
+            tmat(1, 1)
+            xquant(6)
+            mtrans(3)
+            mul(4, 0)
+            exp(5, 0)
+            mquant(2)
+            xtrans(7, 0)
+            mul(4, 1)
+            mexit(3)
+            mtrans(4)
+            xtrans(7, 1)
+            mul(5, 0)
             zrest(6, 0)
-            tcopy(3, 1)
-            mul(6, 1)
-            mexit(5)
-            lossp(2, 0)
+            prod(7, 0)
             zout(6, 0)
-            zrest(7, 0)
+            tcopy(1, 1)
+            exp(5, 1)
+            prod(7, 1)
+            lossp(1, 0)
+            lossp(1, 1)
+            mexit(4)
+            xquant(7)
+            tmat(2, 0)
+            zrest(6, 1)
+            mquant(3)
             exp(6, 0)
-            mquant(5)
-            mul(6, 0)
+            lossp(2, 0)
+            tcopy(2, 0)
+            tmat(2, 1)
+            mul(5, 1)
+            lossp(2, 1)
+            zout(6, 1)
             tmat(3, 0)
-            zout(7, 0)
+            mul(6, 0)
+            mtrans(5)
+            mquant(4)
+            exp(6, 1)
             lossp(3, 0)
-            tmat(4, 0)
+            zrest(7, 0)
+            mexit(5)
+            tmat(3, 1)
+            zout(7, 0)
+            tcopy(2, 1)
+            mul(6, 1)
+            tcopy(3, 0)
             exp(7, 0)
             zrest(7, 1)
-            lossp(4, 0)
-            tcopy(3, 0)
+            tmat(4, 0)
+            lossp(3, 1)
             mul(7, 0)
+            mquant(5)
             zout(7, 1)
-            tcopy(4, 0)
-            mtrans(6)
+            tcopy(3, 1)
             exp(7, 1)
-            tmat(5, 1)
-            tmat(5, 0)
-            mexit(6)
-            mul(7, 1)
+            lossp(4, 0)
             tmat(4, 1)
-            tcopy(5, 1)
+            mtrans(6)
+            lossp(4, 1)
+            tmat(5, 0)
+            mul(7, 1)
+            tmat(5, 1)
+            mexit(6)
             mquant(6)
+            tcopy(4, 0)
             lossp(5, 0)
-            mtrans(7)
             tcopy(4, 1)
-            tmat(6, 1)
+            mtrans(7)
             lossp(5, 1)
             mexit(7)
-            tcopy(5, 0)
-            lossp(4, 1)
-            tmat(6, 0)
-            tcopy(6, 1)
             mquant(7)
+            tmat(6, 0)
             lossp(6, 0)
-            tmat(7, 1)
+            tcopy(5, 0)
+            tmat(6, 1)
             tmat(7, 0)
-            lossp(6, 1)
+            tcopy(5, 1)
             tcopy(6, 0)
-            tcopy(7, 1)
+            lossp(6, 1)
             lossp(7, 0)
+            tcopy(6, 1)
+            tmat(7, 1)
             lossp(7, 1)
             tcopy(7, 0)
+            tcopy(7, 1)
             nc.vector.tensor_tensor(out=lpad[:, 0:NT], in0=acc[0][:], in1=acc[1][:], op=ALU.add)
             lt = psum.tile([P, 2, 2, P], F32, name="xt", tag="xt", bufs=4)
             nc.tensor.transpose(lt[:, 0, 0, :], lpad[:], ident[:])

@@ -84,32 +84,32 @@ def tile_c51_shifted_log_loss_s3_kernel(
                 nc.sync.dma_start(out=xo[a][:], in_=x_out[2 * P * a : 2 * P * (a + 1), :].rearrange("(i r) k -> r i k", r=P))
 
             load_x(0)
-            load_xo(0)
-            load_x(2)
-            nc.sync.dma_start(out=sc[:].rearrange("p g u e -> p g (u e)"), in_=x_rest_scale.rearrange("o (g p t) -> p (o g) t", p=P, t=4))
             load_x(1)
+            load_xo(0)
+            nc.sync.dma_start(out=sc[:].rearrange("p g u e -> p g (u e)"), in_=x_rest_scale.rearrange("o (g p t) -> p (o g) t", p=P, t=4))
             nc.sync.dma_start(out=wraw[:], in_=w_out.rearrange("(p j) n -> p j n", j=4))
+            load_x(2)
             load_onl(0)
             load_xo(1)
-            load_onl(1)
             nc.sync.dma_start(out=base[:], in_=base_words.rearrange("g p n -> p g n"))
             for q in range(4):
                 nc.sync.dma_start(
                     out=bsc[32 * q : 32 * q + 4].bitcast(I32),
                     in_=base_scales[:, 4 * q : 4 * q + 4, :].rearrange("g r n -> r g n").bitcast(I32),
                 )
-            load_onl(2)
+            load_onl(1)
             load_x(3)
-            nc.sync.dma_start(out=spc[:], in_=spacing.partition_broadcast(P))
+            load_onl(2)
             nc.sync.dma_start(out=scb[:], in_=x_rest_scale.rearrange("o k -> (o k)").partition_broadcast(P))
-            load_x(5)
             load_x(4)
-            load_xo(2)
-            load_onl(3)
             load_x(7)
-            load_xo(3)
-            nc.sync.dma_start(out=proj[:], in_=proj_words.rearrange("g p n -> p g n"))
+            load_xo(2)
             load_x(6)
+            load_xo(3)
+            load_onl(3)
+            load_x(5)
+            nc.sync.dma_start(out=spc[:], in_=spacing.partition_broadcast(P))
+            nc.sync.dma_start(out=proj[:], in_=proj_words.rearrange("g p n -> p g n"))
             for q in range(4):
                 nc.sync.dma_start(
                     out=psc[32 * q : 32 * q + 4].bitcast(I32),
@@ -199,14 +199,15 @@ def tile_c51_shifted_log_loss_s3_kernel(
                 )
 
             def wgroup(h):
-                nc.gpsimd.tensor_scalar(
-                    out=wgrp[h][:],
-                    in0=wraw[:, :, HALF * h : HALF * (h + 1)].rearrange("p j n -> p n j"),
-                    scalar1=1.0,
-                    scalar2=0.0,
-                    op0=ALU.mult,
-                    op1=ALU.add,
-                )
+                for c in range(0, HALF, P):
+                    nc.gpsimd.tensor_scalar(
+                        out=wgrp[h][:, c : c + P],
+                        in0=wraw[:, :, HALF * h + c : HALF * h + c + P].rearrange("p j n -> p n j"),
+                        scalar1=1.0,
+                        scalar2=0.0,
+                        op0=ALU.mult,
+                        op1=ALU.add,
+                    )
 
             def wquant(h):
                 nc.vector.quantize_mx(out=wcod[h][:].bitcast(FP8X4), scales=wscl[h][:], in_=wgrp[h][:].rearrange("p n j -> p (n j)"))
@@ -245,15 +246,14 @@ def tile_c51_shifted_log_loss_s3_kernel(
             def mul(i, h):
                 if i not in mass:
                     mass[i] = work.tile([P, GM, 2, P, 2], BF16, name="mass", tag="mass", bufs=3)
+                eng = nc.vector
                 cols = slice(HALF * h, HALF * (h + 1))
-                dst = mass[i][:, h]
-                src = ex[i][:, cols].rearrange("b (p u e) -> b u p e", u=2, e=2)
-                fac = spc[:, cols].rearrange("b (p u e) -> b u p e", u=2, e=2)
-                if i >= 5:
-                    nc.vector.tensor_tensor(out=dst, in0=src, in1=fac, op=ALU.mult)
-                else:
-                    for u in range(2):
-                        nc.gpsimd.tensor_tensor(out=dst[:, u], in0=src[:, u], in1=fac[:, u], op=ALU.mult)
+                eng.tensor_tensor(
+                    out=mass[i][:, h],
+                    in0=ex[i][:, cols].rearrange("b (p u e) -> b u p e", u=2, e=2),
+                    in1=spc[:, cols].rearrange("b (p u e) -> b u p e", u=2, e=2),
+                    op=ALU.mult,
+                )
 
             def mtrans(i):
                 t = psum.tile([P, 2, 2, P], F32, name="xt", tag="xt", bufs=4)
@@ -312,213 +312,213 @@ def tile_c51_shifted_log_loss_s3_kernel(
             def ln(i):
                 nc.scalar.activation(out=logs[:, i, :], in_=onl[i // 2][:, i % 2, :], func=ACT.Ln)
 
-            otrans(0)
             cast(0)
+            wgroup(0)
             xtrans(0, 0)
             cast(1)
-            prod(0, 0)
-            cast(2)
             xtrans(0, 1)
+            prod(0, 0)
+            otrans(0)
             oexit(0)
             xtrans(1, 0)
-            ln(0)
             xtrans(1, 1)
-            ln(1)
-            otrans(1)
             prod(0, 1)
+            oquant(0)
             prod(1, 0)
+            cast(2)
+            ln(0)
+            xquant(0)
             prod(1, 1)
             xtrans(2, 0)
-            oexit(1)
-            xtrans(2, 1)
-            xquant(0)
-            wgroup(0)
-            xquant(1)
-            ln(2)
-            zrest(0, 0)
-            prod(2, 0)
-            oquant(0)
             wquant(0)
-            ln(3)
-            prod(2, 1)
+            xtrans(2, 1)
+            otrans(1)
+            xquant(1)
+            prod(2, 0)
+            ln(1)
+            zrest(0, 0)
+            oexit(1)
             wgroup(1)
+            prod(2, 1)
+            zrest(0, 1)
             wquant(1)
             xquant(2)
-            zrest(0, 1)
-            oquant(1)
             zout(0, 0)
+            ln(2)
+            zrest(1, 0)
+            zout(0, 1)
+            zout(1, 0)
+            zrest(1, 1)
+            zout(1, 1)
+            otrans(2)
+            ln(3)
             cast(3)
             ln(4)
             ln(5)
-            zrest(1, 0)
-            zout(0, 1)
-            cast(4)
-            zrest(1, 1)
+            xtrans(3, 0)
             exp(0, 0)
+            xtrans(3, 1)
+            oquant(1)
+            zrest(2, 0)
             exp(0, 1)
-            zout(1, 0)
-            zout(1, 1)
+            oexit(2)
             exp(1, 0)
             exp(1, 1)
-            zrest(2, 0)
             zout(2, 0)
-            ln(6)
             zrest(2, 1)
-            mul(0, 0)
-            mul(0, 1)
-            otrans(2)
-            xtrans(3, 0)
-            mul(1, 0)
-            zout(2, 1)
+            cast(4)
             cast(5)
-            xtrans(3, 1)
-            oexit(2)
-            xtrans(4, 0)
+            zout(2, 1)
             prod(3, 0)
-            prod(3, 1)
+            xtrans(4, 0)
             xtrans(4, 1)
+            xtrans(5, 0)
+            exp(2, 0)
+            mul(0, 0)
+            prod(3, 1)
+            xtrans(5, 1)
+            exp(2, 1)
+            xquant(3)
             prod(4, 0)
             otrans(3)
-            xtrans(5, 0)
-            mul(1, 1)
-            xquant(3)
-            xtrans(5, 1)
-            prod(4, 1)
-            ln(7)
-            mtrans(0)
             zrest(3, 0)
-            zrest(3, 1)
-            exp(2, 0)
-            exp(2, 1)
-            zout(3, 0)
-            mexit(0)
-            zout(3, 1)
-            cast(6)
-            exp(3, 0)
-            oexit(3)
-            xquant(4)
-            mquant(0)
-            exp(3, 1)
-            zrest(4, 0)
-            zrest(4, 1)
-            mul(2, 0)
-            mul(2, 1)
-            tmat(0, 0)
+            mul(0, 1)
+            prod(4, 1)
             oquant(2)
-            zout(4, 0)
-            mul(3, 0)
+            ln(6)
             prod(5, 0)
-            tmat(0, 1)
-            xtrans(6, 0)
-            tcopy(0, 0)
-            lossp(0, 0)
-            mtrans(1)
-            mul(3, 1)
+            zout(3, 0)
+            mul(1, 0)
+            mul(1, 1)
             prod(5, 1)
+            mul(2, 0)
+            xquant(4)
+            oexit(3)
+            zrest(3, 1)
+            cast(6)
+            mul(2, 1)
+            zrest(4, 0)
+            ln(7)
+            zrest(4, 1)
+            zout(3, 1)
             xquant(5)
+            zout(4, 0)
+            mtrans(0)
+            cast(7)
+            xtrans(6, 0)
+            mtrans(1)
+            exp(3, 0)
+            xtrans(6, 1)
+            mexit(0)
+            mquant(0)
+            mul(3, 0)
+            exp(3, 1)
+            prod(6, 0)
+            mul(3, 1)
+            zrest(5, 0)
             exp(4, 0)
             mexit(1)
-            mtrans(2)
-            xtrans(6, 1)
+            mul(4, 0)
             zout(4, 1)
             mquant(1)
-            prod(6, 0)
-            lossp(0, 1)
-            zrest(5, 0)
-            exp(4, 1)
-            oquant(3)
-            prod(6, 1)
-            cast(7)
-            tcopy(0, 1)
-            mexit(2)
-            zrest(5, 1)
-            tmat(1, 0)
             zout(5, 0)
-            zout(5, 1)
-            tcopy(1, 0)
-            tmat(1, 1)
-            xquant(6)
-            mtrans(3)
-            mul(4, 0)
-            exp(5, 0)
-            mquant(2)
+            tmat(0, 0)
+            prod(6, 1)
             xtrans(7, 0)
-            mul(4, 1)
-            mexit(3)
-            mtrans(4)
-            xtrans(7, 1)
-            mul(5, 0)
-            zrest(6, 0)
+            exp(4, 1)
+            exp(5, 0)
+            mtrans(2)
+            xquant(6)
+            lossp(0, 0)
             prod(7, 0)
-            zout(6, 0)
-            tcopy(1, 1)
-            exp(5, 1)
+            xtrans(7, 1)
+            mexit(2)
+            tcopy(0, 0)
+            mtrans(3)
+            tmat(0, 1)
+            tmat(1, 0)
+            lossp(0, 1)
+            mul(4, 1)
+            zrest(5, 1)
+            oquant(3)
+            mquant(2)
             prod(7, 1)
             lossp(1, 0)
-            lossp(1, 1)
-            mexit(4)
+            tcopy(0, 1)
+            tcopy(1, 0)
+            zout(5, 1)
             xquant(7)
-            tmat(2, 0)
-            zrest(6, 1)
-            mquant(3)
+            zrest(6, 0)
+            tmat(1, 1)
+            zout(6, 0)
+            mul(5, 0)
+            exp(5, 1)
             exp(6, 0)
-            lossp(2, 0)
-            tcopy(2, 0)
-            tmat(2, 1)
             mul(5, 1)
-            lossp(2, 1)
+            lossp(1, 1)
+            tmat(2, 0)
+            mexit(3)
+            zrest(6, 1)
             zout(6, 1)
+            mtrans(4)
+            tcopy(1, 1)
+            exp(6, 1)
+            mexit(4)
+            mquant(3)
+            lossp(2, 0)
+            mtrans(5)
+            tmat(2, 1)
+            tcopy(2, 0)
+            mexit(5)
+            zrest(7, 0)
             tmat(3, 0)
             mul(6, 0)
-            mtrans(5)
+            lossp(2, 1)
             mquant(4)
-            exp(6, 1)
-            lossp(3, 0)
-            zrest(7, 0)
-            mexit(5)
-            tmat(3, 1)
-            zout(7, 0)
-            tcopy(2, 1)
             mul(6, 1)
-            tcopy(3, 0)
+            tmat(3, 1)
+            tcopy(2, 1)
+            lossp(3, 0)
+            zout(7, 0)
             exp(7, 0)
             zrest(7, 1)
-            tmat(4, 0)
-            lossp(3, 1)
-            mul(7, 0)
+            tcopy(3, 0)
             mquant(5)
+            lossp(3, 1)
+            tmat(4, 0)
             zout(7, 1)
-            tcopy(3, 1)
-            exp(7, 1)
+            mul(7, 0)
             lossp(4, 0)
             tmat(4, 1)
-            mtrans(6)
+            tcopy(3, 1)
+            exp(7, 1)
             lossp(4, 1)
-            tmat(5, 0)
+            mtrans(6)
             mul(7, 1)
-            tmat(5, 1)
             mexit(6)
+            tmat(5, 0)
             mquant(6)
+            tmat(5, 1)
             tcopy(4, 0)
             lossp(5, 0)
             tcopy(4, 1)
             mtrans(7)
-            lossp(5, 1)
             mexit(7)
-            mquant(7)
-            tmat(6, 0)
-            lossp(6, 0)
             tcopy(5, 0)
+            lossp(5, 1)
+            tmat(6, 0)
             tmat(6, 1)
-            tmat(7, 0)
             tcopy(5, 1)
+            mquant(7)
+            lossp(6, 0)
+            tmat(7, 0)
             tcopy(6, 0)
-            lossp(6, 1)
-            lossp(7, 0)
-            tcopy(6, 1)
             tmat(7, 1)
-            lossp(7, 1)
+            lossp(6, 1)
+            tcopy(6, 1)
+            lossp(7, 0)
             tcopy(7, 0)
+            lossp(7, 1)
             tcopy(7, 1)
             nc.vector.tensor_tensor(out=lpad[:, 0:NT], in0=acc[0][:], in1=acc[1][:], op=ALU.add)
             lt = psum.tile([P, 2, 2, P], F32, name="xt", tag="xt", bufs=4)

from contextlib import ExitStack

import concourse.mybir as mybir
from concourse.masks import make_identity

B, KO, KR, F, J = 1024, 512, 2048, 1024, 1024
FLOPS = 2 * B * F * (KO + KR) + 2 * B * J * F

F32 = mybir.dt.float32
BF16 = mybir.dt.bfloat16
I32 = mybir.dt.int32
U32 = mybir.dt.uint32
U8 = mybir.dt.uint8
FP8 = mybir.dt.float8_e4m3fn
FP8X4 = mybir.dt.float8_e4m3fn_x4
FP4X4 = mybir.dt.float4_e2m1fn_x4
ACT = mybir.ActivationFunctionType
ALU = mybir.AluOpType

P = 128
NT = B // P
HALF = 512
GR = KR // 512
GM = F // 512


def tile_c51_shifted_log_loss_s3_kernel(
    tc, x_out, w_out, x_rest_bytes, x_rest_scale, base_words, base_scales, spacing, proj_words, proj_scales, online, target, loss
):
    nc = tc.nc
    with ExitStack() as ctx:
        keep = ctx.enter_context(tc.tile_pool(name="keep", bufs=1))
        work = ctx.enter_context(tc.tile_pool(name="work", bufs=3))
        psum = ctx.enter_context(tc.psum_pool(name="psum", bufs=4))

        def kept(shape, dtype, name):
            return keep.tile(shape, dtype, name=name, tag=name, align_bytes=64)

        xr = [kept([P, KR], U8, "xr%d" % i) for i in range(NT)]
        sc = kept([P, GR, 2, 2], F32, "sc")
        base = kept([P, GR, 2 * F], U8, "base")
        scb = kept([P, KR], F32, "scb")
        bsc = kept([P, GR, F], U8, "bsc")
        proj = kept([P, GM, 2 * J], U8, "proj")
        psc = kept([P, GM, J], U8, "psc")
        wraw = kept([P, 4, F], BF16, "wraw")
        wgrp = [kept([P, HALF, 4], BF16, "wgrp%d" % h) for h in range(2)]
        wcod = [kept([P, HALF], U32, "wcod%d" % h) for h in range(2)]
        wscl = [kept([P, HALF], U8, "wscl%d" % h) for h in range(2)]
        xo = [kept([P, 2, KO], BF16, "xo%d" % i) for i in range(NT // 2)]
        onl = [kept([P, 2, J], BF16, "onl%d" % i) for i in range(NT // 2)]
        logs = kept([P, NT, J], F32, "logs")
        spc = kept([P, F], BF16, "spc")
        ident = kept([P, P], F32, "ident")
        acc = [kept([P, NT], F32, "acc%d" % h) for h in range(2)]
        lpad = kept([P, P], F32, "lpad")
        lrow = kept([32, P], F32, "lrow")
        one = kept([P, 1], F32, "one")
        junk1 = kept([P, 1], F32, "junk1")
        xcod = [kept([P, GR, P], U32, "xcod%d" % i) for i in range(NT)]
        xscl = [kept([P, GR, P], U8, "xscl%d" % i) for i in range(NT)]
        ocod = [kept([P, 2, P], U32, "ocod%d" % i) for i in range(NT // 2)]
        oscl = [kept([P, 2, P], U8, "oscl%d" % i) for i in range(NT // 2)]

        with tc.manual_schedule():
            nc.vector.memset(one[:], 1.0)
            nc.vector.memset(bsc[:].rearrange("p g n -> p (g n)").bitcast(I32), 0)
            nc.vector.memset(psc[:].rearrange("p g n -> p (g n)").bitcast(I32), 0)
            nc.vector.memset(lpad[:], 0.0)
            nc.scalar.activation(out=junk1[:], in_=one[:], func=ACT.Ln)
            make_identity(nc, ident[:])

            def load_x(i):
                if i == 0:
                    nc.sync.dma_start(out=xr[i][:, 0:1024], in_=x_rest_bytes[0:P, 0:1024])
                    nc.sync.dma_start(out=xr[i][:, 1024:2048], in_=x_rest_bytes[0:P, 1024:2048])
                    return
                nc.sync.dma_start(out=xr[i][:], in_=x_rest_bytes[P * i : P * (i + 1), :])

            def load_onl(a):
                nc.sync.dma_start(out=onl[a][:], in_=online[2 * P * a : 2 * P * (a + 1), :].rearrange("(i r) j -> r i j", r=P))

            def load_xo(a):
                nc.sync.dma_start(out=xo[a][:], in_=x_out[2 * P * a : 2 * P * (a + 1), :].rearrange("(i r) k -> r i k", r=P))

            load_x(0)
            load_x(1)
            load_xo(0)
            nc.sync.dma_start(out=sc[:].rearrange("p g u e -> p g (u e)"), in_=x_rest_scale.rearrange("o (g p t) -> p (o g) t", p=P, t=4))
            nc.sync.dma_start(out=wraw[:], in_=w_out.rearrange("(p j) n -> p j n", j=4))
            load_x(2)
            load_onl(0)
            load_xo(1)
            nc.sync.dma_start(out=base[:], in_=base_words.rearrange("g p n -> p g n"))
            for q in range(4):
                nc.sync.dma_start(
                    out=bsc[32 * q : 32 * q + 4].bitcast(I32),
                    in_=base_scales[:, 4 * q : 4 * q + 4, :].rearrange("g r n -> r g n").bitcast(I32),
                )
            load_onl(1)
            load_x(3)
            load_onl(2)
            nc.sync.dma_start(out=scb[:], in_=x_rest_scale.rearrange("o k -> (o k)").partition_broadcast(P))
            load_x(4)
            load_x(7)
            load_xo(2)
            load_x(6)
            load_xo(3)
            load_onl(3)
            load_x(5)
            nc.sync.dma_start(out=spc[:], in_=spacing.partition_broadcast(P))
            nc.sync.dma_start(out=proj[:], in_=proj_words.rearrange("g p n -> p g n"))
            for q in range(4):
                nc.sync.dma_start(
                    out=psc[32 * q : 32 * q + 4].bitcast(I32),
                    in_=proj_scales[:, 4 * q : 4 * q + 4, :].rearrange("g r n -> r g n").bitcast(I32),
                )

            wide = {}
            xt = {}
            grp = {}
            z = {}
            ex = {}
            mass = {}
            mt = {}
            mgrp = {}
            mcod = {}
            mscl = {}
            tg = {}
            tout = {}

            def cast(i):
                if i in (3, 4, 5, 6, 7,):
                    t = work.tile([P, KR], BF16, name="wide", tag="wide", bufs=4)
                    wide[i] = t
                    nc.vector.tensor_tensor(out=t[:], in0=xr[i][:].bitcast(FP8), in1=scb[:], op=ALU.mult)
                    return
                t = work.tile([P, KR], BF16, name="wide", tag="wide", bufs=4)
                wide[i] = t
                if i == 0:
                    for c in (0, 1024):
                        nc.scalar.copy(out=t[:, c : c + 512], in_=xr[i][:, c : c + 512].bitcast(FP8))
                        nc.vector.tensor_copy(out=t[:, c + 512 : c + 1024], in_=xr[i][:, c + 512 : c + 1024].bitcast(FP8))
                elif i == 1:
                    nc.scalar.copy(out=t[:, 0:1024], in_=xr[i][:, 0:1024].bitcast(FP8))
                    nc.vector.tensor_copy(out=t[:, 1024:2048], in_=xr[i][:, 1024:2048].bitcast(FP8))
                else:
                    nc.scalar.copy(out=t[:], in_=xr[i][:].bitcast(FP8))

            def xtrans(i, b):
                t = psum.tile([P, 2, 2, P], F32, name="xt", tag="xt", bufs=4)
                xt[i, b] = t
                words = wide[i][:].bitcast(F32)
                for gg in range(2):
                    g = 2 * b + gg
                    for u in range(2):
                        nc.tensor.transpose(t[:, u, gg, :], words[:, 256 * g + u : 256 * (g + 1) : 2], ident[:])

            def prod(i, b):
                if i not in grp:
                    grp[i] = work.tile([P, GR, P, 2, 2], BF16, name="grp", tag="grp", bufs=4, align_bytes=64)
                if i in (3, 4, 5, 6, 7,):
                    nc.scalar.copy(
                        out=grp[i][:, 2 * b : 2 * b + 2].rearrange("p g r u e -> p (g r u e)").bitcast(F32).rearrange("p (g r u) -> p g r u", g=2, u=2),
                        in_=xt[i, b][:].rearrange("p u g r -> p g r u"),
                    )
                    return
                t = xt[i, b][:].rearrange("p u g r -> p (u g r)").bitcast(BF16).rearrange("p (u g r e) -> p g r u e", u=2, g=2, e=2)
                s = sc[:, 2 * b : 2 * b + 2].unsqueeze(2).to_broadcast([P, 2, P, 2, 2])
                nc.vector.tensor_tensor(out=grp[i][:, 2 * b : 2 * b + 2], in0=t, in1=s, op=ALU.mult)

            def xquant(i):
                nc.vector.quantize_mx(
                    out=xcod[i][:].rearrange("p g r -> p (g r)").bitcast(FP8X4),
                    scales=xscl[i][:].rearrange("p g r -> p (g r)"),
                    in_=grp[i][:].rearrange("p g r u e -> p (g r u e)"),
                )

            def otrans(a):
                t = psum.tile([P, 2, 2, P], F32, name="xt", tag="xt", bufs=4)
                xt["o", a] = t
                for i in range(2):
                    words = xo[a][:, i, :].bitcast(F32)
                    for u in range(2):
                        nc.tensor.transpose(t[:, u, i, :], words[:, u::2], ident[:])

            def oexit(a):
                grp["o", a] = work.tile([P, 2 * P * 4], BF16, name="ogrp", tag="ogrp", bufs=2, align_bytes=64)
                nc.scalar.copy(
                    out=grp["o", a][:].bitcast(F32).rearrange("p (i r u) -> p i r u", i=2, u=2),
                    in_=xt["o", a][:].rearrange("p u i r -> p i r u"),
                )

            def oquant(a):
                nc.vector.quantize_mx(
                    out=ocod[a][:].rearrange("p i r -> p (i r)").bitcast(FP8X4),
                    scales=oscl[a][:].rearrange("p i r -> p (i r)"),
                    in_=grp["o", a][:],
                )

            def wgroup(h):
                for c in range(0, HALF, P):
                    nc.gpsimd.tensor_scalar(
                        out=wgrp[h][:, c : c + P],
                        in0=wraw[:, :, HALF * h + c : HALF * h + c + P].rearrange("p j n -> p n j"),
                        scalar1=1.0,
                        scalar2=0.0,
                        op0=ALU.mult,
                        op1=ALU.add,
                    )

            def wquant(h):
                nc.vector.quantize_mx(out=wcod[h][:].bitcast(FP8X4), scales=wscl[h][:], in_=wgrp[h][:].rearrange("p n j -> p (n j)"))

            def zrest(i, h):
                t = psum.tile([P, HALF], F32, name="mm", tag="mm", bufs=4)
                z[i, h] = t
                for g in range(GR):
                    nc.tensor.matmul_mx(
                        out=t[:],
                        lhsT=xcod[i][:, g, :].bitcast(FP8X4),
                        lhsT_scale=xscl[i][:, g, :],
                        rhs=base[:, g, 2 * HALF * h : 2 * HALF * (h + 1)].bitcast(FP4X4),
                        rhs_scale=bsc[:, g, HALF * h : HALF * (h + 1)],
                        start=(g == 0),
                        stop=False,
                    )

            def zout(i, h):
                a, j = i // 2, i % 2
                nc.tensor.matmul_mx(
                    out=z[i, h][:],
                    lhsT=ocod[a][:, j, :].bitcast(FP8X4),
                    lhsT_scale=oscl[a][:, j, :],
                    rhs=wcod[h][:].bitcast(FP8X4),
                    rhs_scale=wscl[h][:],
                    start=False,
                    stop=True,
                )

            def exp(i, h):
                if i not in ex:
                    ex[i] = work.tile([P, F], F32, name="ex", tag="ex", bufs=3)
                nc.scalar.activation(out=ex[i][:, HALF * h : HALF * (h + 1)], in_=z[i, h][:], func=ACT.Exp)

            def mul(i, h):
                if i not in mass:
                    mass[i] = work.tile([P, GM, 2, P, 2], BF16, name="mass", tag="mass", bufs=3)
                eng = nc.vector
                cols = slice(HALF * h, HALF * (h + 1))
                eng.tensor_tensor(
                    out=mass[i][:, h],
                    in0=ex[i][:, cols].rearrange("b (p u e) -> b u p e", u=2, e=2),
                    in1=spc[:, cols].rearrange("b (p u e) -> b u p e", u=2, e=2),
                    op=ALU.mult,
                )

            def mtrans(i):
                t = psum.tile([P, 2, 2, P], F32, name="xt", tag="xt", bufs=4)
                mt[i] = t
                for g in range(GM):
                    for u in range(2):
                        nc.tensor.transpose(t[:, u, g, :], mass[i][:, g, u].rearrange("b p e -> b (p e)").bitcast(F32), ident[:])

            def mexit(i):
                mgrp[i] = work.tile([P, GM * P * 4], BF16, name="mgrp", tag="mgrp", bufs=2, align_bytes=64)
                nc.scalar.copy(
                    out=mgrp[i][:].bitcast(F32).rearrange("p (g b u) -> p g b u", g=GM, u=2),
                    in_=mt[i][:].rearrange("p u g b -> p g b u"),
                )

            def mquant(i):
                mcod[i] = work.tile([P, GM, P], U32, name="mcod", tag="mcod", bufs=3, align_bytes=64)
                mscl[i] = work.tile([P, GM, P], U8, name="mscl", tag="mscl", bufs=3, align_bytes=64)
                nc.vector.quantize_mx(
                    out=mcod[i][:].rearrange("p g b -> p (g b)").bitcast(FP8X4),
                    scales=mscl[i][:].rearrange("p g b -> p (g b)"),
                    in_=mgrp[i][:],
                )

            def tmat(i, h):
                t = psum.tile([P, HALF], F32, name="mm", tag="mm", bufs=4)
                tg[i, h] = t
                for g in range(GM):
                    nc.tensor.matmul_mx(
                        out=t[:],
                        lhsT=mcod[i][:, g, :].bitcast(FP8X4),
                        lhsT_scale=mscl[i][:, g, :],
                        rhs=proj[:, g, 2 * HALF * h : 2 * HALF * (h + 1)].bitcast(FP4X4),
                        rhs_scale=psc[:, g, HALF * h : HALF * (h + 1)],
                        start=(g == 0),
                        stop=(g == GM - 1),
                    )

            def tcopy(i, h):
                half = work.tile([P, HALF], F32, name="tout", tag="tout", bufs=8)
                nc.scalar.copy(out=half[:], in_=tg[i, h][:])
                nc.sync.dma_start(out=target[P * i : P * (i + 1), HALF * h : HALF * (h + 1)], in_=half[:])

            def lossp(i, h):
                prods = work.tile([P, HALF], F32, name="prods", tag="prods", bufs=2)
                nc.vector.scalar_tensor_tensor(
                    out=prods[:],
                    in0=tg[i, h][:],
                    scalar=-1.0 / J,
                    in1=logs[:, i, HALF * h : HALF * (h + 1)],
                    op0=ALU.mult,
                    op1=ALU.mult,
                    accum_out=acc[h][:, i : i + 1],
                )

            def ln(i):
                nc.scalar.activation(out=logs[:, i, :], in_=onl[i // 2][:, i % 2, :], func=ACT.Ln)

            cast(0)
            wgroup(0)
            xtrans(0, 0)
            cast(1)
            xtrans(0, 1)
            prod(0, 0)
            otrans(0)
            oexit(0)
            xtrans(1, 0)
            xtrans(1, 1)
            prod(0, 1)
            oquant(0)
            prod(1, 0)
            cast(2)
            ln(0)
            xquant(0)
            prod(1, 1)
            xtrans(2, 0)
            wquant(0)
            xtrans(2, 1)
            otrans(1)
            xquant(1)
            prod(2, 0)
            ln(1)
            zrest(0, 0)
            oexit(1)
            wgroup(1)
            prod(2, 1)
            zrest(0, 1)
            wquant(1)
            xquant(2)
            zout(0, 0)
            ln(2)
            zrest(1, 0)
            zout(0, 1)
            zout(1, 0)
            zrest(1, 1)
            zout(1, 1)
            otrans(2)
            ln(3)
            cast(3)
            ln(4)
            ln(5)
            xtrans(3, 0)
            exp(0, 0)
            xtrans(3, 1)
            oquant(1)
            zrest(2, 0)
            exp(0, 1)
            oexit(2)
            exp(1, 0)
            exp(1, 1)
            zout(2, 0)
            zrest(2, 1)
            cast(4)
            cast(5)
            zout(2, 1)
            prod(3, 0)
            xtrans(4, 0)
            xtrans(4, 1)
            xtrans(5, 0)
            exp(2, 0)
            mul(0, 0)
            prod(3, 1)
            xtrans(5, 1)
            exp(2, 1)
            xquant(3)
            prod(4, 0)
            otrans(3)
            zrest(3, 0)
            mul(0, 1)
            prod(4, 1)
            oquant(2)
            ln(6)
            prod(5, 0)
            zout(3, 0)
            mul(1, 0)
            mul(1, 1)
            prod(5, 1)
            mul(2, 0)
            xquant(4)
            oexit(3)
            zrest(3, 1)
            cast(6)
            mul(2, 1)
            zrest(4, 0)
            ln(7)
            zrest(4, 1)
            zout(3, 1)
            xquant(5)
            zout(4, 0)
            mtrans(0)
            cast(7)
            xtrans(6, 0)
            mtrans(1)
            exp(3, 0)
            xtrans(6, 1)
            mexit(0)
            mquant(0)
            mul(3, 0)
            exp(3, 1)
            prod(6, 0)
            mul(3, 1)
            zrest(5, 0)
            exp(4, 0)
            mexit(1)
            mul(4, 0)
            zout(4, 1)
            mquant(1)
            zout(5, 0)
            tmat(0, 0)
            prod(6, 1)
            xtrans(7, 0)
            exp(4, 1)
            exp(5, 0)
            mtrans(2)
            xquant(6)
            lossp(0, 0)
            prod(7, 0)
            xtrans(7, 1)
            mexit(2)
            tcopy(0, 0)
            mtrans(3)
            tmat(0, 1)
            tmat(1, 0)
            lossp(0, 1)
            mul(4, 1)
            zrest(5, 1)
            oquant(3)
            mquant(2)
            prod(7, 1)
            lossp(1, 0)
            tcopy(0, 1)
            tcopy(1, 0)
            zout(5, 1)
            xquant(7)
            zrest(6, 0)
            tmat(1, 1)
            zout(6, 0)
            mul(5, 0)
            exp(5, 1)
            exp(6, 0)
            mul(5, 1)
            lossp(1, 1)
            tmat(2, 0)
            mexit(3)
            zrest(6, 1)
            zout(6, 1)
            mtrans(4)
            tcopy(1, 1)
            exp(6, 1)
            mexit(4)
            mquant(3)
            lossp(2, 0)
            mtrans(5)
            tmat(2, 1)
            tcopy(2, 0)
            mexit(5)
            zrest(7, 0)
            tmat(3, 0)
            mul(6, 0)
            lossp(2, 1)
            mquant(4)
            mul(6, 1)
            tmat(3, 1)
            tcopy(2, 1)
            lossp(3, 0)
            zout(7, 0)
            exp(7, 0)
            zrest(7, 1)
            tcopy(3, 0)
            mquant(5)
            lossp(3, 1)
            tmat(4, 0)
            zout(7, 1)
            mul(7, 0)
            lossp(4, 0)
            tmat(4, 1)
            tcopy(3, 1)
            exp(7, 1)
            lossp(4, 1)
            mtrans(6)
            mul(7, 1)
            mexit(6)
            tmat(5, 0)
            mquant(6)
            tmat(5, 1)
            tcopy(4, 0)
            lossp(5, 0)
            tcopy(4, 1)
            mtrans(7)
            mexit(7)
            tcopy(5, 0)
            lossp(5, 1)
            tmat(6, 0)
            tmat(6, 1)
            tcopy(5, 1)
            mquant(7)
            lossp(6, 0)
            tmat(7, 0)
            tcopy(6, 0)
            tmat(7, 1)
            lossp(6, 1)
            tcopy(6, 1)
            lossp(7, 0)
            tcopy(7, 0)
            lossp(7, 1)
            tcopy(7, 1)
            nc.vector.tensor_tensor(out=lpad[:, 0:NT], in0=acc[0][:], in1=acc[1][:], op=ALU.add)
            lt = psum.tile([P, 2, 2, P], F32, name="xt", tag="xt", bufs=4)
            nc.tensor.transpose(lt[:, 0, 0, :], lpad[:], ident[:])
            nc.scalar.copy(out=lrow[:], in_=lt[0:32, 0, 0, :])
            nc.sync.dma_start(out=loss.rearrange("(i b) -> i b", b=P), in_=lrow[0:NT, :])
